import numpy as np
import ml_dtypes


def mxq(x, axis, fmt="e4m3"):
    dtype, down = {"e4m3": (ml_dtypes.float8_e4m3fn, 7), "e5m2": (ml_dtypes.float8_e5m2, 14)}[fmt]
    v = np.moveaxis(np.asarray(x, np.float32).astype(ml_dtypes.bfloat16).astype(np.float64), axis, -1)
    blocks = v.reshape(v.shape[:-1] + (-1, 32))
    amax = np.abs(blocks).max(-1, keepdims=True)
    byte = np.maximum(np.where(amax > 0, np.frexp(amax)[1] - 1 + 127, 0) - down, 1)
    scale = np.exp2(byte - 127.0)
    codes = (blocks / scale).astype(np.float32).astype(dtype).astype(np.float64)
    return np.moveaxis((codes * scale).reshape(v.shape), -1, axis)


WIDE = False


def mx_kscale(k):
    if not WIDE:
        return np.ones(k)
    levels = np.array([10, -10, 5, -5, 0])
    if k % 512:
        return np.exp2(np.random.permutation(np.resize(levels, k // 32))).repeat(32)
    a = np.empty((k // 512, 16))
    for p in range(k // 512):
        a[p, :8] = np.random.permutation(np.resize(levels, 8))
        for g in range(8):
            far = levels[np.abs(levels - a[p, g]) >= 10]
            a[p, g + 8] = far[np.random.randint(len(far))]
    return np.exp2(a.ravel()).repeat(32)


BF16 = ml_dtypes.bfloat16


def bf(x):
    return np.asarray(x, np.float32).astype(BF16)


def f64(x):
    return np.asarray(x).astype(np.float64)


E2M1 = np.array([0.0, 0.5, 1.0, 1.5, 2.0, 3.0, 4.0, 6.0, -0.0, -0.5, -1.0, -1.5, -2.0, -3.0, -4.0, -6.0])


def pack_weight(w, fmt):
    k, n = w.shape
    w = f64(bf(w)).reshape(k // 32, 32, n)
    amax = np.abs(w).max(1)
    if fmt == "e4m3":
        byte = np.frexp(amax)[1] - 1 + 127 - 7
    else:
        mant, ex = np.frexp(amax / 6.0)
        byte = np.where(mant > 0.5, ex, ex - 1) + 127
    byte = np.clip(np.where(amax > 0, byte, 1), 1, 254)
    scaled = (w * np.exp2(127.0 - byte)[:, None, :]).reshape(k, n).astype(np.float32)
    by_word = np.ascontiguousarray(scaled.reshape(k // 512, 128, 4, n).transpose(0, 1, 3, 2))
    if fmt == "e4m3":
        words = by_word.astype(ml_dtypes.float8_e4m3fn).view(np.uint8)
    else:
        c = by_word.astype(ml_dtypes.float4_e2m1fn).view(np.uint8) & 0xF
        words = c[..., 0::2] | (c[..., 1::2] << 4)
    return np.ascontiguousarray(words), np.ascontiguousarray(byte.astype(np.uint8).reshape(k // 512, 16, n))


def unpack_weight(words, scales, fmt):
    g, p, n, _ = words.shape
    if fmt == "e4m3":
        vals = np.ascontiguousarray(words).view(ml_dtypes.float8_e4m3fn).astype(np.float64)
    else:
        nib = np.empty((g, p, n, 4), np.uint8)
        nib[..., 0::2] = words & 0xF
        nib[..., 1::2] = words >> 4
        vals = E2M1[nib]
    vals = vals * np.repeat(np.exp2(scales.astype(np.float64) - 127.0), 8, axis=1)[..., None]
    return vals.transpose(0, 1, 3, 2).reshape(g * 512, n)
def pack4(w):
    words, scales = pack_weight(w, "e2m1")
    return words.reshape(words.shape[0], 128, -1), scales


def unpack4(words, scales):
    return unpack_weight(words.reshape(words.shape[0], 128, -1, 2), scales, "e2m1")


E4M3FN = np.array([(-1.0 if i & 128 else 1.0) * ((1.0 + (i & 7) / 8.0) * 2.0 ** (((i >> 3) & 15) - 7) if i & 120 else (i & 7) * 2.0 ** -9) for i in range(256)])


def e4m3fn_bytes(y):
    return np.clip(np.asarray(y, np.float64), -448.0, 448.0).astype(np.float32).astype(ml_dtypes.float8_e4m3fn).view(np.uint8)


def e4m3fn_values(b):
    return E4M3FN[b]


N, D, F, H = 1024, 1024, 1024, 2
HEAD_GAIN = np.array([2.0, 1.0])
P_HIT = 0.3


def softplus(v):
    return np.maximum(v, 0.0) + np.log(1.0 + np.exp(-np.abs(v)))


def draw0():
    r, t = mx_kscale(D), mx_kscale(F)
    x = bf(np.random.standard_normal((N, D)))
    xbar = bf(np.random.standard_normal((N, D)))
    u = bf(np.random.uniform(0.0, 1.0, (N, D)))
    s = bf((1.0 + 0.1 * np.random.standard_normal(D)) * r)
    we_words, we_scales = pack4(np.random.standard_normal((D, F)) / np.sqrt(D) / r[:, None])
    return {"x": x,
            "xbar": xbar,
            "u": u,
            "s": s,
            "we_words": we_words,
            "we_scales": we_scales,
            "g": bf((1.0 + 0.1 * np.random.standard_normal(F)) * t),
            "wh": bf(np.random.standard_normal((H, F, D)) * HEAD_GAIN[:, None, None] / np.sqrt(F) / t[None, :, None])}


def corrupt(x, xbar, u, s):
    hit = u < P_HIT
    m = np.where(hit, 1.0, 0.0)
    xt = s[None, :] * np.where(hit, xbar, x)
    return m, xt


def encode(xt, we, g):
    return g[None, :] * np.tanh(mxq(xt, 1, "e4m3") @ we)


def core(x, xbar, u, s, we_words, we_scales, g, wh):
    x, xbar, u, s, g, wh = f64(x), f64(xbar), f64(u), f64(s), f64(g), f64(wh)
    we = unpack4(we_words, we_scales)
    m, xt = corrupt(x, xbar, u, s)
    h = encode(xt, we, g)
    hq = mxq(h, 1, "e4m3")
    whq = mxq(wh, 1, "e4m3")
    a = hq @ whq[0]
    rec = hq @ whq[1]
    return softplus(a) - m * a + 2.0 * np.square(rec - x)


def setup_inputs():
    drawn = draw0()
    full = np.asarray(drawn['wh']).astype(np.float64)
    scale = (np.abs(full).reshape(2, 1024, 8, 128).max(axis=(3,)) / 448.0).astype(np.float32)
    given = {}
    for key, value in drawn.items():
        if key == 'wh':
            given['wh_bytes'] = e4m3fn_bytes(full / np.repeat(scale.astype(np.float64), 128, axis=2))
            given['wh_scale'] = scale
        else:
            given[key] = value
    return given


def reference(x, xbar, u, s, we_words, we_scales, g, wh_bytes, wh_scale):
    return core(x, xbar, u, s, we_words, we_scales, g, e4m3fn_values(wh_bytes) * np.repeat(wh_scale.astype(np.float64), 128, axis=2))

@@ -1,0 +1,390 @@
+from contextlib import ExitStack
+
+import concourse.mybir as mybir
+from concourse.masks import make_identity
+
+F32 = mybir.dt.float32
+BF16 = mybir.dt.bfloat16
+I32 = mybir.dt.int32
+U32 = mybir.dt.uint32
+U8 = mybir.dt.uint8
+F8 = mybir.dt.float8_e4m3fn
+FP8X4 = mybir.dt.float8_e4m3fn_x4
+FP4X4 = mybir.dt.float4_e2m1fn_x4
+ALU = mybir.AluOpType
+ACT = mybir.ActivationFunctionType
+
+P = 128
+N = 1024
+D = 1024
+F = 1024
+NT = N // P
+NP = NT // 2
+P_HIT = 0.3
+LN_FLOOR = 1e-13
+FLOPS = 3 * 2 * N * D * F
+
+V_WI = (4, 5)
+WSD_BUFS = 3
+
+
+def tile_vimemaskandfeaturepretextloss_d1p_kernel(tc, x, xbar, u, s, we_words, we_scales, g, wh_bytes, wh_scale, out):
+    nc = tc.nc
+    with ExitStack() as ctx:
+        keep = ctx.enter_context(tc.tile_pool(name="keep", bufs=1))
+        work = ctx.enter_context(tc.tile_pool(name="work", bufs=2))
+        psum = ctx.enter_context(tc.psum_pool(name="psum", bufs=2))
+        ctx.enter_context(tc.manual_schedule())
+
+        ident = keep.tile([P, P], F32, name="ident")
+        ones = keep.tile([P, P], BF16, name="ones")
+        srow = keep.tile([P, D], BF16, name="srow")
+        s_b = keep.tile([P, D], BF16, name="s_b")
+        g_col = keep.tile([P, 2, 4], BF16, name="g_col")
+        wsca = keep.tile([P, 2, 2, 32], F32, name="wsca")
+        wew = keep.tile([P, 2, 2048], U8, name="wew", align_bytes=64)
+        wep = keep.tile([P, 2, 2048], U8, name="wep", align_bytes=64)
+        wsc = keep.tile([P, 2, 1024], U8, name="wsc", align_bytes=64)
+        wsp = keep.tile([P, 2, 1024], U8, name="wsp", align_bytes=64)
+        xs = [keep.tile([P, 2, D], BF16, name="x%d" % i) for i in range(NP)]
+        ms = [keep.tile([P, 2, D], BF16, name="m%d" % i) for i in range(NP)]
+        xc = [keep.tile([P, 256], U32, name="xc%d" % i, align_bytes=64) for i in range(NT)]
+        xsc = [keep.tile([P, 256], U8, name="xsc%d" % i, align_bytes=64) for i in range(NT)]
+        hc = [keep.tile([P, 256], U32, name="hc%d" % i, align_bytes=64) for i in range(NT)]
+        hsc = [keep.tile([P, 256], U8, name="hsc%d" % i, align_bytes=64) for i in range(NT)]
+        whc = [keep.tile([P, 2, 1024], U32, name="whc%d" % h, align_bytes=64) for h in range(2)]
+        whs = [keep.tile([P, 2, 1024], U8, name="whs%d" % h, align_bytes=64) for h in range(2)]
+        cs = [keep.tile([P, 2, D], F32, name="c%d" % i) for i in range(NP)]
+        sg = [keep.tile([P, 2, D], F32, name="sg%d" % i) for i in range(NP)]
+        slab = [work.tile([P, 2, 2, D], BF16, name="slab", bufs=NP) for i in range(NP)]
+        warm = keep.tile([P, 1], F32, name="warm")
+
+        nc.vector.memset(warm[:], 0.0)
+        nc.scalar.activation(out=warm[:], in_=warm[:], func=ACT.Sigmoid)
+        nc.gpsimd.memset(srow[:], 0.0)
+        nc.gpsimd.memset(ones[:], 1.0)
+        nc.gpsimd.memset(wsc[:].bitcast(I32), 0)
+        make_identity(nc, ident[:])
+
+        wb = {}
+
+        def load_tok(i, count=1):
+            q, r = i // 2, i % 2
+            part = slice(r, r + count)
+            rows = slice(i * P, (i + count) * P)
+            for dst, src in ((slab[q][:, 0, part], u), (xs[q][:, part], x), (slab[q][:, 1, part], xbar)):
+                nc.sync.dma_start(out=dst, in_=src[rows, :].rearrange("(r p) d -> p r d", p=P))
+
+        def load_wh(h, gg):
+            wb[h, gg] = work.tile([P, 4, 1024], U8, name="wb", bufs=3)
+            nc.sync.dma_start(
+                out=wb[h, gg][:].rearrange("p t n -> p (t n)"),
+                in_=wh_bytes[h].rearrange("(g p t) n -> g p (t n)", p=P, t=4)[gg],
+            )
+
+        load_tok(0)
+        nc.sync.dma_start(out=wsca[:], in_=wh_scale.rearrange("h (g p t) j -> p h g (t j)", p=P, t=4))
+        nc.sync.dma_start(out=srow[0:1, :], in_=s.rearrange("(o d) -> o d", o=1))
+        load_wh(0, 0)
+        load_tok(1)
+        load_tok(2, 2)
+        load_wh(0, 1)
+        nc.sync.dma_start(out=wew[:], in_=we_words.rearrange("g p b -> p g b"))
+        for q in range(4):
+            nc.sync.dma_start(
+                out=wsc[32 * q : 32 * q + 4, :, :].bitcast(I32),
+                in_=we_scales.bitcast(I32)[:, 4 * q : 4 * q + 4, :].rearrange("g r n -> r g n"),
+            )
+        nc.sync.dma_start(out=g_col[:], in_=g.rearrange("(g p t) -> p g t", p=P, t=4))
+        load_tok(4, 2)
+        load_wh(1, 0)
+        load_tok(6, 2)
+        load_wh(1, 1)
+
+        for c in range(2):
+            sp = psum.tile([P, 512], F32, name="acc", bufs=4)
+            nc.tensor.matmul(sp[:], lhsT=ones[:], rhs=srow[:, 512 * c : 512 * c + 512], start=True, stop=True)
+            nc.scalar.copy(out=s_b[:, 512 * c : 512 * c + 512], in_=sp[:])
+
+        xg = {}
+        pieces = [(0, slice(0, 1)), (0, slice(1, 2))] + [(q, slice(0, 2)) for q in range(1, NP)]
+
+        def views(k):
+            q, r = pieces[k]
+            return slab[q][:, 0, r], slab[q][:, 1, r], xs[q][:, r], ms[q][:, r]
+
+        def mask_m(k):
+            uu, bb, xx, mm = views(k)
+            nc.vector.tensor_scalar(out=mm, in0=uu, scalar1=P_HIT, scalar2=None, op0=ALU.is_lt)
+
+        def mask_n(k):
+            uu, bb, xx, mm = views(k)
+            nc.vector.tensor_scalar(out=uu, in0=uu, scalar1=P_HIT, scalar2=None, op0=ALU.is_ge)
+
+        def prod_a(k):
+            uu, bb, xx, mm = views(k)
+            nc.vector.tensor_tensor(out=bb, in0=mm, in1=bb, op=ALU.mult)
+
+        def prod_b(k):
+            uu, bb, xx, mm = views(k)
+            nc.vector.tensor_tensor(out=uu, in0=uu, in1=xx, op=ALU.mult)
+
+        def add_ab(k):
+            uu, bb, xx, mm = views(k)
+            nc.vector.tensor_tensor(out=uu, in0=uu, in1=bb, op=ALU.add)
+
+        def mul_s(k):
+            uu, bb, xx, mm = views(k)
+            q, r = pieces[k]
+            nc.vector.tensor_tensor(out=uu, in0=uu, in1=s_b[:].unsqueeze(1).to_broadcast([P, r.stop - r.start, D]), op=ALU.mult)
+
+        def turn(i):
+            bank = psum.tile([P, 4, P], F32, name="turned", bufs=2)
+            words = slab[i // 2][:, 0, i % 2].bitcast(F32)
+            for gg in range(2):
+                for v in range(2):
+                    nc.tensor.transpose(bank[:, 2 * gg + v, :], words[:, 256 * gg + v : 256 * (gg + 1) : 2], ident[:])
+            xg[i] = work.tile([P, 2, P, 4], BF16, name="xg", bufs=2, align_bytes=64)
+            nc.scalar.copy(
+                out=xg[i][:].rearrange("p g r t -> p (g r t)").bitcast(F32).rearrange("p (g r v) -> p g r v", g=2, v=2),
+                in_=bank[:].rearrange("p (g v) r -> p g r v", g=2),
+            )
+
+        def quant_x(i):
+            nc.vector.quantize_mx(out=xc[i][:].bitcast(FP8X4), scales=xsc[i][:], in_=xg[i][:].rearrange("p g r t -> p (g r t)"))
+
+        def permute_we(t):
+            nc.vector.tensor_copy(
+                out=wep[:].rearrange("p g (h t m b) -> p (g h) t m b", h=2, t=4, b=2)[:, :, t],
+                in_=wew[:].rearrange("p g (h m t b) -> p (g h) t m b", h=2, t=4, b=2)[:, :, t],
+            )
+
+        def permute_ws(t):
+            nc.vector.tensor_copy(
+                out=wsp[:].rearrange("p g (h t m) -> p (g h) t m", h=2, t=4)[:, :, t],
+                in_=wsc[:].rearrange("p g (h m t) -> p (g h) t m", h=2, t=4)[:, :, t],
+            )
+
+        units = [(0, 0, 0), (0, 0, 1), (0, 1, 0), (0, 1, 1), (1, 0, 0), (1, 1, 0), (1, 0, 1), (1, 1, 1)]
+        wsd = {}
+        wil = {}
+
+        def widen(k, part):
+            h, gg, nh = units[k]
+            if part == 0:
+                wsd[k] = work.tile([P, 4, 512], BF16, name="wsd", bufs=WSD_BUFS)
+            for t in (2 * part, 2 * part + 1):
+                for j in range(4):
+                    col = 8 * t + 4 * nh + j
+                    nc.scalar.activation(
+                        out=wsd[k][:, t, 128 * j : 128 * j + 128],
+                        in_=wb[h, gg][:, t, 512 * nh + 128 * j : 512 * nh + 128 * j + 128].bitcast(F8),
+                        func=ACT.Copy,
+                        scale=wsca[:, h, gg, col : col + 1],
+                    )
+
+        def interleave(k, part):
+            if part == 0:
+                wil[k] = work.tile([P, 512, 4], BF16, name="wil", bufs=2, align_bytes=64)
+            cols = slice(256 * part, 256 * part + 256)
+            dst = wil[k][:, cols, :]
+            src = wsd[k][:, :, cols].rearrange("p t n -> p n t")
+            if k in V_WI:
+                nc.vector.tensor_copy(out=dst, in_=src)
+            else:
+                nc.scalar.copy(out=dst, in_=src)
+
+        def inter_v(k):
+            interleave(k, 0)
+            interleave(k, 1)
+            quant_w(k)
+
+        def quant_w(k):
+            h, gg, nh = units[k]
+            cols = slice(512 * nh, 512 * nh + 512)
+            nc.vector.quantize_mx(out=whc[h][:, gg, cols].bitcast(FP8X4), scales=whs[h][:, gg, cols], in_=wil[k][:].rearrange("p n t -> p (n t)"))
+
+        y1 = {}
+        th = {}
+        hg = {}
+
+        def mm1(i):
+            for gg in range(2):
+                y1[i, gg] = psum.tile([P, 4, P], F32, name="y1", bufs=2)
+                for t in range(4):
+                    c0 = 512 * gg + 128 * t
+                    for k in range(2):
+                        nc.tensor.matmul_mx(
+                            out=y1[i, gg][:, t, :],
+                            lhsT=wep[:, k, 2 * c0 : 2 * c0 + 256].bitcast(FP4X4),
+                            lhsT_scale=wsp[:, k, c0 : c0 + 128],
+                            rhs=xc[i][:, 128 * k : 128 * k + 128].bitcast(FP8X4),
+                            rhs_scale=xsc[i][:, 128 * k : 128 * k + 128],
+                            start=(k == 0),
+                            stop=(k == 1),
+                        )
+
+        def tanh(i):
+            th[i] = work.tile([P, 2, P, 4], F32, name="th", bufs=2)
+            for gg in range(2):
+                nc.scalar.activation(out=th[i][:, gg], in_=y1[i, gg][:].rearrange("p t r -> p r t"), func=ACT.Tanh)
+
+        def mul_g(i):
+            hg[i] = work.tile([P, 2, P, 4], BF16, name="hg", bufs=2, align_bytes=64)
+            nc.vector.tensor_tensor(
+                out=hg[i][:], in0=th[i][:], in1=g_col[:].unsqueeze(2).to_broadcast([P, 2, P, 4]), op=ALU.mult
+            )
+
+        def quant_h(i):
+            nc.vector.quantize_mx(out=hc[i][:].bitcast(FP8X4), scales=hsc[i][:], in_=hg[i][:].rearrange("p g r t -> p (g r t)"))
+
+        acc = {}
+
+        def mm2(i, h, nh):
+            acc[i, h, nh] = psum.tile([P, 512], F32, name="acc", bufs=4)
+            cols = slice(512 * nh, 512 * nh + 512)
+            for gg in range(2):
+                ks = slice(128 * gg, 128 * gg + 128)
+                nc.tensor.matmul_mx(
+                    out=acc[i, h, nh][:],
+                    lhsT=hc[i][:, ks].bitcast(FP8X4),
+                    lhsT_scale=hsc[i][:, ks],
+                    rhs=whc[h][:, gg, cols].bitcast(FP8X4),
+                    rhs_scale=whs[h][:, gg, cols],
+                    start=(gg == 0),
+                    stop=(gg == 1),
+                )
+
+        def flip(i, nh):
+            cols = slice(512 * nh, 512 * nh + 512)
+            nc.vector.scalar_tensor_tensor(
+                out=cs[i // 2][:, i % 2, cols], in0=ms[i // 2][:, i % 2, cols], scalar=0.5, in1=acc[i, 0, nh][:], op0=ALU.subtract, op1=ALU.mult
+            )
+
+        def sigm(q, r):
+            nc.scalar.activation(out=sg[q][:, r], in_=cs[q][:, r], func=ACT.Sigmoid, scale=2.0)
+
+        dt = {}
+
+        def diff(i, nh):
+            cols = slice(512 * nh, 512 * nh + 512)
+            nc.vector.tensor_tensor(
+                out=dt[i // 2][:, i % 2, cols], in0=acc[i, 1, nh][:], in1=xs[i // 2][:, i % 2, cols], op=ALU.subtract
+            )
+
+        def log(q, r):
+            nc.scalar.activation(out=sg[q][:, r], in_=sg[q][:, r], func=ACT.Ln, bias=LN_FLOOR)
+
+        def sqr(q, r):
+            nc.scalar.activation(out=dt[q][:, r], in_=dt[q][:, r], func=ACT.Square)
+
+        def mini(q, r, c=slice(0, D)):
+            nc.vector.scalar_tensor_tensor(out=cs[q][:, r, c], in0=cs[q][:, r, c], scalar=2.0, in1=sg[q][:, r, c], op0=ALU.mult, op1=ALU.min)
+
+        def fin(q, r, c=slice(0, D)):
+            nc.vector.scalar_tensor_tensor(out=dt[q][:, r, c], in0=dt[q][:, r, c], scalar=2.0, in1=cs[q][:, r, c], op0=ALU.mult, op1=ALU.subtract)
+            rows = slice((2 * q + r.start) * P, (2 * q + r.stop) * P)
+            nc.sync.dma_start(out=out[rows, c].rearrange("(r p) d -> p r d", p=P), in_=dt[q][:, r, c])
+
+        def ok(i):
+            return 0 <= i < NT
+
+        ALL = slice(0, 2)
+        ONE = (slice(0, 1), slice(1, 2))
+
+        def s_item(kind, unit):
+            for part in range(2):
+                if kind == "w":
+                    widen(unit, part)
+                else:
+                    interleave(unit, part)
+
+        tiles_of = [(0,), (1,), (2, 3), (4, 5), (6, 7)]
+        fill_s = [[("w", 0)], [("w", 1)], [("i", 0), ("i", 1)], [("w", 2), ("w", 3)], [("i", 2), ("i", 3)], [("w", 4)], []]
+        fill_v = {2: [(permute_we, t) for t in range(4)], 3: [(permute_ws, t) for t in range(4)] + [(quant_w, 0), (quant_w, 1)], 6: [(quant_w, 2), (quant_w, 3)]}
+        NK = len(pieces)
+        for k in range(NK + 2):
+            for kind, unit in fill_s[k]:
+                s_item(kind, unit)
+            if k < NK:
+                mask_m(k)
+            if 1 <= k <= NK:
+                add_ab(k - 1)
+            if k < NK:
+                mask_n(k)
+            if 1 <= k <= NK:
+                mul_s(k - 1)
+                for i in tiles_of[k - 1]:
+                    turn(i)
+            if k < NK:
+                prod_a(k)
+            if 2 <= k:
+                for i in tiles_of[k - 2]:
+                    if i < 6:
+                        quant_x(i)
+            for f, a in fill_v.get(k, []):
+                f(a)
+            if k < NK:
+                prod_b(k)
+            if k == 4:
+                mm1(0)
+                tanh(0)
+                mm1(1)
+
+        todo_s = [(widen, k, p) for k in (5, 6, 7) for p in range(2)] + [(interleave, k, p) for k in (6, 7) for p in range(2)] + [(sigm, q, ALL) for q in range(NP)]
+        n_s = [1, 1, 1, 1, 1, 1, 1, 1, 2]
+        v_b = {3: [(inter_v, 4)], 5: [(inter_v, 5)]}
+        pos = [0]
+        for j in range(NT + 1):
+            if ok(j + 1):
+                tanh(j + 1)
+            for i in range(6, NT):
+                if j == i - 6:
+                    quant_x(i)
+            if ok(j + 2):
+                mm1(j + 2)
+            if ok(j):
+                mul_g(j)
+            if ok(j - 1):
+                flip(j - 1, 0)
+            if ok(j):
+                quant_h(j)
+            if ok(j - 1):
+                flip(j - 1, 1)
+            if ok(j):
+                mm2(j, 0, 0)
+                mm2(j, 0, 1)
+            for f, a in v_b.get(j, []):
+                f(a)
+            for f, a, b in todo_s[pos[0] : pos[0] + n_s[j]]:
+                f(a, b)
+            pos[0] += n_s[j]
+        for f, a, b in todo_s[pos[0] :]:
+            f(a, b)
+        for q in range(NP):
+            dt[q] = work.tile([P, 2, D], F32, name="slab", bufs=NP)
+        for i in range(NT):
+            mm2(i, 1, 0)
+            diff(i, 0)
+        quant_w(6)
+        quant_w(7)
+        for i in range(NT):
+            mm2(i, 1, 1)
+            diff(i, 1)
+        for q in range(NP):
+            for r in ONE:
+                log(q, r)
+                sqr(q, r)
+        for q in range(NP):
+            mini(q, ONE[0])
+            if q:
+                fin(q - 1, ONE[1])
+            if q < NP - 1:
+                mini(q, ONE[1])
+                fin(q, ONE[0])
+        halves = (slice(0, D // 2), slice(D // 2, D))
+        mini(NP - 1, ONE[1], halves[0])
+        fin(NP - 1, ONE[0])
+        mini(NP - 1, ONE[1], halves[1])
+        for c in halves:
+            fin(NP - 1, ONE[1], c)

@@ -24,7 +24,7 @@ P_HIT = 0.3
 LN_FLOOR = 1e-13
 FLOPS = 3 * 2 * N * D * F
 
-V_WI = (4, 5)
+V_WI = (5,)
 WSD_BUFS = 3
 
 
@@ -68,24 +68,25 @@ def tile_vimemaskandfeaturepretextloss_d1p_kernel(tc, x, xbar, u, s, we_words, w
 
         wb = {}
 
-        def load_tok(i, count=1):
+        def load_tok(i, count=1, c=slice(0, D)):
             q, r = i // 2, i % 2
             part = slice(r, r + count)
             rows = slice(i * P, (i + count) * P)
-            for dst, src in ((slab[q][:, 0, part], u), (xs[q][:, part], x), (slab[q][:, 1, part], xbar)):
-                nc.sync.dma_start(out=dst, in_=src[rows, :].rearrange("(r p) d -> p r d", p=P))
+            for dst, src in ((slab[q][:, 0, part, c], u), (xs[q][:, part, c], x), (slab[q][:, 1, part, c], xbar)):
+                nc.sync.dma_start(out=dst, in_=src[rows, c].rearrange("(r p) d -> p r d", p=P))
 
-        def load_wh(h, gg):
-            wb[h, gg] = work.tile([P, 4, 1024], U8, name="wb", bufs=3)
-            nc.sync.dma_start(
-                out=wb[h, gg][:].rearrange("p t n -> p (t n)"),
-                in_=wh_bytes[h].rearrange("(g p t) n -> g p (t n)", p=P, t=4)[gg],
-            )
+        def load_wh(h, gg, ts=slice(0, 4)):
+            if ts.start == 0:
+                wb[h, gg] = work.tile([P, 4, 1024], U8, name="wb", bufs=3)
+            nc.sync.dma_start(out=wb[h, gg][:, ts, :], in_=wh_bytes[h].rearrange("(g p t) n -> g p t n", p=P, t=4)[gg][:, ts, :])
 
-        load_tok(0)
+        half = (slice(0, D // 2), slice(D // 2, D))
+        load_tok(0, 1, half[0])
         nc.sync.dma_start(out=wsca[:], in_=wh_scale.rearrange("h (g p t) j -> p h g (t j)", p=P, t=4))
         nc.sync.dma_start(out=srow[0:1, :], in_=s.rearrange("(o d) -> o d", o=1))
-        load_wh(0, 0)
+        load_wh(0, 0, slice(0, 2))
+        load_tok(0, 1, half[1])
+        load_wh(0, 0, slice(2, 4))
         load_tok(1)
         load_tok(2, 2)
         load_wh(0, 1)
@@ -101,17 +102,18 @@ def tile_vimemaskandfeaturepretextloss_d1p_kernel(tc, x, xbar, u, s, we_words, w
         load_tok(6, 2)
         load_wh(1, 1)
 
-        for c in range(2):
+        def spread_s(c):
             sp = psum.tile([P, 512], F32, name="acc", bufs=4)
-            nc.tensor.matmul(sp[:], lhsT=ones[:], rhs=srow[:, 512 * c : 512 * c + 512], start=True, stop=True)
-            nc.scalar.copy(out=s_b[:, 512 * c : 512 * c + 512], in_=sp[:])
+            nc.tensor.matmul(sp[:], lhsT=ones[:], rhs=srow[:, half[c]], start=True, stop=True)
+            nc.scalar.copy(out=s_b[:, half[c]], in_=sp[:])
 
         xg = {}
-        pieces = [(0, slice(0, 1)), (0, slice(1, 2))] + [(q, slice(0, 2)) for q in range(1, NP)]
+        FULL = slice(0, D)
+        pieces = [(0, slice(0, 1), half[0]), (0, slice(0, 1), half[1]), (0, slice(1, 2), FULL)] + [(q, slice(0, 2), FULL) for q in range(1, NP)]
 
         def views(k):
-            q, r = pieces[k]
-            return slab[q][:, 0, r], slab[q][:, 1, r], xs[q][:, r], ms[q][:, r]
+            q, r, c = pieces[k]
+            return slab[q][:, 0, r, c], slab[q][:, 1, r, c], xs[q][:, r, c], ms[q][:, r, c]
 
         def mask_m(k):
             uu, bb, xx, mm = views(k)
@@ -135,8 +137,10 @@ def tile_vimemaskandfeaturepretextloss_d1p_kernel(tc, x, xbar, u, s, we_words, w
 
         def mul_s(k):
             uu, bb, xx, mm = views(k)
-            q, r = pieces[k]
-            nc.vector.tensor_tensor(out=uu, in0=uu, in1=s_b[:].unsqueeze(1).to_broadcast([P, r.stop - r.start, D]), op=ALU.mult)
+            q, r, c = pieces[k]
+            nc.vector.tensor_tensor(
+                out=uu, in0=uu, in1=s_b[:, c].unsqueeze(1).to_broadcast([P, r.stop - r.start, c.stop - c.start]), op=ALU.mult
+            )
 
         def turn(i):
             bank = psum.tile([P, 4, P], F32, name="turned", bufs=2)
@@ -187,8 +191,8 @@ def tile_vimemaskandfeaturepretextloss_d1p_kernel(tc, x, xbar, u, s, we_words, w
             if part == 0:
                 wil[k] = work.tile([P, 512, 4], BF16, name="wil", bufs=2, align_bytes=64)
             cols = slice(256 * part, 256 * part + 256)
-            dst = wil[k][:, cols, :]
-            src = wsd[k][:, :, cols].rearrange("p t n -> p n t")
+            dst = wil[k][:, cols, :].rearrange("p (c i) t -> p c t i", i=4)
+            src = wsd[k][:, :, cols].rearrange("p t (c i) -> p c t i", i=4)
             if k in V_WI:
                 nc.vector.tensor_copy(out=dst, in_=src)
             else:
@@ -292,20 +296,19 @@ def tile_vimemaskandfeaturepretextloss_d1p_kernel(tc, x, xbar, u, s, we_words, w
         ALL = slice(0, 2)
         ONE = (slice(0, 1), slice(1, 2))
 
-        def s_item(kind, unit):
-            for part in range(2):
-                if kind == "w":
-                    widen(unit, part)
-                else:
-                    interleave(unit, part)
-
-        tiles_of = [(0,), (1,), (2, 3), (4, 5), (6, 7)]
-        fill_s = [[("w", 0)], [("w", 1)], [("i", 0), ("i", 1)], [("w", 2), ("w", 3)], [("i", 2), ("i", 3)], [("w", 4)], []]
-        fill_v = {2: [(permute_we, t) for t in range(4)], 3: [(permute_ws, t) for t in range(4)] + [(quant_w, 0), (quant_w, 1)], 6: [(quant_w, 2), (quant_w, 3)]}
+        tiles_of = [(), (0,), (1,), (2, 3), (4, 5), (6, 7)]
+        W = [[(widen, k, p) for p in range(2)] for k in range(8)]
+        I = [[(interleave, k, p) for p in range(2)] for k in range(8)]
+        fill_s = [[], W[0][1:], W[1], I[0] + I[1], W[2] + W[3], I[2] + I[3] + W[4], I[4][:1], []]
+        fill_v = {3: [(permute_we, t) for t in range(4)], 4: [(permute_ws, t) for t in range(4)] + [(quant_w, 0), (quant_w, 1)], 7: [(quant_w, 2), (quant_w, 3)]}
         NK = len(pieces)
         for k in range(NK + 2):
-            for kind, unit in fill_s[k]:
-                s_item(kind, unit)
+            if k == 0:
+                widen(0, 0)
+                spread_s(0)
+                spread_s(1)
+            for f, a, b in fill_s[k]:
+                f(a, b)
             if k < NK:
                 mask_m(k)
             if 1 <= k <= NK:
@@ -326,14 +329,14 @@ def tile_vimemaskandfeaturepretextloss_d1p_kernel(tc, x, xbar, u, s, we_words, w
                 f(a)
             if k < NK:
                 prod_b(k)
-            if k == 4:
+            if k == 5:
                 mm1(0)
                 tanh(0)
                 mm1(1)
 
-        todo_s = [(widen, k, p) for k in (5, 6, 7) for p in range(2)] + [(interleave, k, p) for k in (6, 7) for p in range(2)] + [(sigm, q, ALL) for q in range(NP)]
+        todo_s = I[4][1:] + W[5] + W[6] + W[7] + I[6] + I[7] + [(sigm, q, ALL) for q in range(NP)]
         n_s = [1, 1, 1, 1, 1, 1, 1, 1, 2]
-        v_b = {3: [(inter_v, 4)], 5: [(inter_v, 5)]}
+        v_b = {2: [(quant_w, 4)], 4: [(inter_v, 5)]}
         pos = [0]
         for j in range(NT + 1):
             if ok(j + 1):

@@ -24,7 +24,7 @@ P_HIT = 0.3
 LN_FLOOR = 1e-13
 FLOPS = 3 * 2 * N * D * F
 
-V_WI = (5,)
+V_WI = ()
 WSD_BUFS = 3
 
 
@@ -191,8 +191,8 @@ def tile_vimemaskandfeaturepretextloss_d1p_kernel(tc, x, xbar, u, s, we_words, w
             if part == 0:
                 wil[k] = work.tile([P, 512, 4], BF16, name="wil", bufs=2, align_bytes=64)
             cols = slice(256 * part, 256 * part + 256)
-            dst = wil[k][:, cols, :].rearrange("p (c i) t -> p c t i", i=4)
-            src = wsd[k][:, :, cols].rearrange("p t (c i) -> p c t i", i=4)
+            dst = wil[k][:, cols, :].rearrange("p (c i) t -> p c t i", i=8)
+            src = wsd[k][:, :, cols].rearrange("p t (c i) -> p c t i", i=8)
             if k in V_WI:
                 nc.vector.tensor_copy(out=dst, in_=src)
             else:
@@ -295,20 +295,32 @@ def tile_vimemaskandfeaturepretextloss_d1p_kernel(tc, x, xbar, u, s, we_words, w
 
         ALL = slice(0, 2)
         ONE = (slice(0, 1), slice(1, 2))
-
         tiles_of = [(), (0,), (1,), (2, 3), (4, 5), (6, 7)]
         W = [[(widen, k, p) for p in range(2)] for k in range(8)]
         I = [[(interleave, k, p) for p in range(2)] for k in range(8)]
-        fill_s = [[], W[0][1:], W[1], I[0] + I[1], W[2] + W[3], I[2] + I[3] + W[4], I[4][:1], []]
-        fill_v = {3: [(permute_we, t) for t in range(4)], 4: [(permute_ws, t) for t in range(4)] + [(quant_w, 0), (quant_w, 1)], 7: [(quant_w, 2), (quant_w, 3)]}
+        PLAN = {'seq': [('i', 0), ('w', 1), ('i', 1), ('w', 2), ('w', 4), ('w', 3), ('i', 2), ('w', 5), ('i', 3), ('i', 5), ('i', 4), ('w', 6), ('w', 7), ('i', 6), ('i', 7)], 'nA': [0, 2, 3, 4, 2, 5, 3, 0], 'nB': [1, 1, 2, 1, 1, 2, 2, 2, 2, 3], 'qA': {7: [2, 3], 5: [1], 3: [0]}, 'qB': {3: [4], 4: [5], 8: [6]}, 'qC': ((), (7,)), 'kT': 5, 'late': 6, 'lag': 2}
+        todo = W[0][1:]
+        for kind, k in PLAN["seq"]:
+            if kind == "w":
+                todo += W[k]
+            elif kind == "i":
+                todo += I[k]
+        todo += [(sigm, q, ALL) for q in range(NP)]
+        pos = [0]
+
+        def scalar_work(count):
+            for f, a, b in todo[pos[0] : pos[0] + count]:
+                f(a, b)
+            pos[0] += count
+
         NK = len(pieces)
+        LATE = PLAN["late"]
         for k in range(NK + 2):
             if k == 0:
                 widen(0, 0)
                 spread_s(0)
                 spread_s(1)
-            for f, a, b in fill_s[k]:
-                f(a, b)
+            scalar_work(PLAN["nA"][k])
             if k < NK:
                 mask_m(k)
             if 1 <= k <= NK:
@@ -323,54 +335,58 @@ def tile_vimemaskandfeaturepretextloss_d1p_kernel(tc, x, xbar, u, s, we_words, w
                 prod_a(k)
             if 2 <= k:
                 for i in tiles_of[k - 2]:
-                    if i < 6:
+                    if i < LATE:
                         quant_x(i)
-            for f, a in fill_v.get(k, []):
-                f(a)
+            if k == 3:
+                for t in range(4):
+                    permute_we(t)
+            if k == 4:
+                for t in range(4):
+                    permute_ws(t)
+            for q in PLAN["qA"].get(k, []):
+                quant_w(q)
             if k < NK:
                 prod_b(k)
-            if k == 5:
+            if k == PLAN["kT"]:
                 mm1(0)
                 tanh(0)
                 mm1(1)
 
-        todo_s = I[4][1:] + W[5] + W[6] + W[7] + I[6] + I[7] + [(sigm, q, ALL) for q in range(NP)]
-        n_s = [1, 1, 1, 1, 1, 1, 1, 1, 2]
-        v_b = {2: [(quant_w, 4)], 4: [(inter_v, 5)]}
-        pos = [0]
-        for j in range(NT + 1):
+        LAG = PLAN["lag"]
+        for j in range(NT + LAG):
             if ok(j + 1):
                 tanh(j + 1)
-            for i in range(6, NT):
-                if j == i - 6:
-                    quant_x(i)
+            if LATE + j < NT:
+                quant_x(LATE + j)
             if ok(j + 2):
                 mm1(j + 2)
             if ok(j):
                 mul_g(j)
-            if ok(j - 1):
-                flip(j - 1, 0)
+            if ok(j - LAG):
+                flip(j - LAG, 0)
             if ok(j):
                 quant_h(j)
-            if ok(j - 1):
-                flip(j - 1, 1)
+            if ok(j - LAG):
+                flip(j - LAG, 1)
             if ok(j):
                 mm2(j, 0, 0)
                 mm2(j, 0, 1)
-            for f, a in v_b.get(j, []):
-                f(a)
-            for f, a, b in todo_s[pos[0] : pos[0] + n_s[j]]:
-                f(a, b)
-            pos[0] += n_s[j]
-        for f, a, b in todo_s[pos[0] :]:
-            f(a, b)
+            for q in PLAN["qB"].get(j, []):
+                if q in V_WI:
+                    interleave(q, 0)
+                    interleave(q, 1)
+                quant_w(q)
+            scalar_work(PLAN["nB"][j])
+        scalar_work(len(todo))
         for q in range(NP):
             dt[q] = work.tile([P, 2, D], F32, name="slab", bufs=NP)
+        for q in PLAN["qC"][0]:
+            quant_w(q)
         for i in range(NT):
             mm2(i, 1, 0)
             diff(i, 0)
-        quant_w(6)
-        quant_w(7)
+        for q in PLAN["qC"][1]:
+            quant_w(q)
         for i in range(NT):
             mm2(i, 1, 1)
             diff(i, 1)
@@ -389,5 +405,5 @@ def tile_vimemaskandfeaturepretextloss_d1p_kernel(tc, x, xbar, u, s, we_words, w
         mini(NP - 1, ONE[1], halves[0])
         fin(NP - 1, ONE[0])
         mini(NP - 1, ONE[1], halves[1])
-        for c in halves:
+        for c in (halves[0], slice(D // 2, 3 * D // 4), slice(3 * D // 4, D)):
             fin(NP - 1, ONE[1], c)

from contextlib import ExitStack

import concourse.mybir as mybir
from concourse.masks import make_identity

F32 = mybir.dt.float32
BF16 = mybir.dt.bfloat16
I32 = mybir.dt.int32
U32 = mybir.dt.uint32
U8 = mybir.dt.uint8
F8 = mybir.dt.float8_e4m3fn
FP8X4 = mybir.dt.float8_e4m3fn_x4
FP4X4 = mybir.dt.float4_e2m1fn_x4
ALU = mybir.AluOpType
ACT = mybir.ActivationFunctionType

P = 128
N = 1024
D = 1024
F = 1024
NT = N // P
NP = NT // 2
P_HIT = 0.3
LN_FLOOR = 1e-13
FLOPS = 3 * 2 * N * D * F

V_WI = ()
WSD_BUFS = 3


def tile_vimemaskandfeaturepretextloss_d1p_kernel(tc, x, xbar, u, s, we_words, we_scales, g, wh_bytes, wh_scale, out):
    nc = tc.nc
    with ExitStack() as ctx:
        keep = ctx.enter_context(tc.tile_pool(name="keep", bufs=1))
        work = ctx.enter_context(tc.tile_pool(name="work", bufs=2))
        psum = ctx.enter_context(tc.psum_pool(name="psum", bufs=2))
        ctx.enter_context(tc.manual_schedule())

        ident = keep.tile([P, P], F32, name="ident")
        ones = keep.tile([P, P], BF16, name="ones")
        srow = keep.tile([P, D], BF16, name="srow")
        s_b = keep.tile([P, D], BF16, name="s_b")
        g_col = keep.tile([P, 2, 4], BF16, name="g_col")
        wsca = keep.tile([P, 2, 2, 32], F32, name="wsca")
        wew = keep.tile([P, 2, 2048], U8, name="wew", align_bytes=64)
        wep = keep.tile([P, 2, 2048], U8, name="wep", align_bytes=64)
        wsc = keep.tile([P, 2, 1024], U8, name="wsc", align_bytes=64)
        wsp = keep.tile([P, 2, 1024], U8, name="wsp", align_bytes=64)
        xs = [keep.tile([P, 2, D], BF16, name="x%d" % i) for i in range(NP)]
        ms = [keep.tile([P, 2, D], BF16, name="m%d" % i) for i in range(NP)]
        xc = [keep.tile([P, 256], U32, name="xc%d" % i, align_bytes=64) for i in range(NT)]
        xsc = [keep.tile([P, 256], U8, name="xsc%d" % i, align_bytes=64) for i in range(NT)]
        hc = [keep.tile([P, 256], U32, name="hc%d" % i, align_bytes=64) for i in range(NT)]
        hsc = [keep.tile([P, 256], U8, name="hsc%d" % i, align_bytes=64) for i in range(NT)]
        whc = [keep.tile([P, 2, 1024], U32, name="whc%d" % h, align_bytes=64) for h in range(2)]
        whs = [keep.tile([P, 2, 1024], U8, name="whs%d" % h, align_bytes=64) for h in range(2)]
        cs = [keep.tile([P, 2, D], F32, name="c%d" % i) for i in range(NP)]
        sg = [keep.tile([P, 2, D], F32, name="sg%d" % i) for i in range(NP)]
        slab = [work.tile([P, 2, 2, D], BF16, name="slab", bufs=NP) for i in range(NP)]
        warm = keep.tile([P, 1], F32, name="warm")

        nc.vector.memset(warm[:], 0.0)
        nc.scalar.activation(out=warm[:], in_=warm[:], func=ACT.Sigmoid)
        nc.gpsimd.memset(srow[:], 0.0)
        nc.gpsimd.memset(ones[:], 1.0)
        nc.gpsimd.memset(wsc[:].bitcast(I32), 0)
        make_identity(nc, ident[:])

        wb = {}

        def load_tok(i, count=1, c=slice(0, D)):
            q, r = i // 2, i % 2
            part = slice(r, r + count)
            rows = slice(i * P, (i + count) * P)
            for dst, src in ((slab[q][:, 0, part, c], u), (xs[q][:, part, c], x), (slab[q][:, 1, part, c], xbar)):
                nc.sync.dma_start(out=dst, in_=src[rows, c].rearrange("(r p) d -> p r d", p=P))

        def load_wh(h, gg, ts=slice(0, 4)):
            if ts.start == 0:
                wb[h, gg] = work.tile([P, 4, 1024], U8, name="wb", bufs=3)
            nc.sync.dma_start(out=wb[h, gg][:, ts, :], in_=wh_bytes[h].rearrange("(g p t) n -> g p t n", p=P, t=4)[gg][:, ts, :])

        half = (slice(0, D // 2), slice(D // 2, D))
        load_tok(0, 1, half[0])
        nc.sync.dma_start(out=wsca[:], in_=wh_scale.rearrange("h (g p t) j -> p h g (t j)", p=P, t=4))
        nc.sync.dma_start(out=srow[0:1, :], in_=s.rearrange("(o d) -> o d", o=1))
        load_wh(0, 0, slice(0, 2))
        load_tok(0, 1, half[1])
        load_wh(0, 0, slice(2, 4))
        load_tok(1)
        load_tok(2, 2)
        load_wh(0, 1)
        nc.sync.dma_start(out=wew[:], in_=we_words.rearrange("g p b -> p g b"))
        for q in range(4):
            nc.sync.dma_start(
                out=wsc[32 * q : 32 * q + 4, :, :].bitcast(I32),
                in_=we_scales.bitcast(I32)[:, 4 * q : 4 * q + 4, :].rearrange("g r n -> r g n"),
            )
        nc.sync.dma_start(out=g_col[:], in_=g.rearrange("(g p t) -> p g t", p=P, t=4))
        load_tok(4, 2)
        load_wh(1, 0)
        load_tok(6, 2)
        load_wh(1, 1)

        def spread_s(c):
            sp = psum.tile([P, 512], F32, name="acc", bufs=4)
            nc.tensor.matmul(sp[:], lhsT=ones[:], rhs=srow[:, half[c]], start=True, stop=True)
            nc.scalar.copy(out=s_b[:, half[c]], in_=sp[:])

        xg = {}
        FULL = slice(0, D)
        pieces = [(0, slice(0, 1), half[0]), (0, slice(0, 1), half[1]), (0, slice(1, 2), FULL)] + [(q, slice(0, 2), FULL) for q in range(1, NP)]

        def views(k):
            q, r, c = pieces[k]
            return slab[q][:, 0, r, c], slab[q][:, 1, r, c], xs[q][:, r, c], ms[q][:, r, c]

        def mask_m(k):
            uu, bb, xx, mm = views(k)
            nc.vector.tensor_scalar(out=mm, in0=uu, scalar1=P_HIT, scalar2=None, op0=ALU.is_lt)

        def mask_n(k):
            uu, bb, xx, mm = views(k)
            nc.vector.tensor_scalar(out=uu, in0=uu, scalar1=P_HIT, scalar2=None, op0=ALU.is_ge)

        def prod_a(k):
            uu, bb, xx, mm = views(k)
            nc.vector.tensor_tensor(out=bb, in0=mm, in1=bb, op=ALU.mult)

        def prod_b(k):
            uu, bb, xx, mm = views(k)
            nc.vector.tensor_tensor(out=uu, in0=uu, in1=xx, op=ALU.mult)

        def add_ab(k):
            uu, bb, xx, mm = views(k)
            nc.vector.tensor_tensor(out=uu, in0=uu, in1=bb, op=ALU.add)

        def mul_s(k):
            uu, bb, xx, mm = views(k)
            q, r, c = pieces[k]
            nc.vector.tensor_tensor(
                out=uu, in0=uu, in1=s_b[:, c].unsqueeze(1).to_broadcast([P, r.stop - r.start, c.stop - c.start]), op=ALU.mult
            )

        def turn(i):
            bank = psum.tile([P, 4, P], F32, name="turned", bufs=2)
            words = slab[i // 2][:, 0, i % 2].bitcast(F32)
            for gg in range(2):
                for v in range(2):
                    nc.tensor.transpose(bank[:, 2 * gg + v, :], words[:, 256 * gg + v : 256 * (gg + 1) : 2], ident[:])
            xg[i] = work.tile([P, 2, P, 4], BF16, name="xg", bufs=2, align_bytes=64)
            nc.scalar.copy(
                out=xg[i][:].rearrange("p g r t -> p (g r t)").bitcast(F32).rearrange("p (g r v) -> p g r v", g=2, v=2),
                in_=bank[:].rearrange("p (g v) r -> p g r v", g=2),
            )

        def quant_x(i):
            nc.vector.quantize_mx(out=xc[i][:].bitcast(FP8X4), scales=xsc[i][:], in_=xg[i][:].rearrange("p g r t -> p (g r t)"))

        def permute_we(t):
            nc.vector.tensor_copy(
                out=wep[:].rearrange("p g (h t m b) -> p (g h) t m b", h=2, t=4, b=2)[:, :, t],
                in_=wew[:].rearrange("p g (h m t b) -> p (g h) t m b", h=2, t=4, b=2)[:, :, t],
            )

        def permute_ws(t):
            nc.vector.tensor_copy(
                out=wsp[:].rearrange("p g (h t m) -> p (g h) t m", h=2, t=4)[:, :, t],
                in_=wsc[:].rearrange("p g (h m t) -> p (g h) t m", h=2, t=4)[:, :, t],
            )

        units = [(0, 0, 0), (0, 0, 1), (0, 1, 0), (0, 1, 1), (1, 0, 0), (1, 1, 0), (1, 0, 1), (1, 1, 1)]
        wsd = {}
        wil = {}

        def widen(k, part):
            h, gg, nh = units[k]
            if part == 0:
                wsd[k] = work.tile([P, 4, 512], BF16, name="wsd", bufs=WSD_BUFS)
            for t in (2 * part, 2 * part + 1):
                for j in range(4):
                    col = 8 * t + 4 * nh + j
                    nc.scalar.activation(
                        out=wsd[k][:, t, 128 * j : 128 * j + 128],
                        in_=wb[h, gg][:, t, 512 * nh + 128 * j : 512 * nh + 128 * j + 128].bitcast(F8),
                        func=ACT.Copy,
                        scale=wsca[:, h, gg, col : col + 1],
                    )

        def interleave(k, part):
            if part == 0:
                wil[k] = work.tile([P, 512, 4], BF16, name="wil", bufs=2, align_bytes=64)
            cols = slice(256 * part, 256 * part + 256)
            dst = wil[k][:, cols, :].rearrange("p (c i) t -> p c t i", i=8)
            src = wsd[k][:, :, cols].rearrange("p t (c i) -> p c t i", i=8)
            if k in V_WI:
                nc.vector.tensor_copy(out=dst, in_=src)
            else:
                nc.scalar.copy(out=dst, in_=src)

        def inter_v(k):
            interleave(k, 0)
            interleave(k, 1)
            quant_w(k)

        def quant_w(k):
            h, gg, nh = units[k]
            cols = slice(512 * nh, 512 * nh + 512)
            nc.vector.quantize_mx(out=whc[h][:, gg, cols].bitcast(FP8X4), scales=whs[h][:, gg, cols], in_=wil[k][:].rearrange("p n t -> p (n t)"))

        y1 = {}
        th = {}
        hg = {}

        def mm1(i):
            for gg in range(2):
                y1[i, gg] = psum.tile([P, 4, P], F32, name="y1", bufs=2)
                for t in range(4):
                    c0 = 512 * gg + 128 * t
                    for k in range(2):
                        nc.tensor.matmul_mx(
                            out=y1[i, gg][:, t, :],
                            lhsT=wep[:, k, 2 * c0 : 2 * c0 + 256].bitcast(FP4X4),
                            lhsT_scale=wsp[:, k, c0 : c0 + 128],
                            rhs=xc[i][:, 128 * k : 128 * k + 128].bitcast(FP8X4),
                            rhs_scale=xsc[i][:, 128 * k : 128 * k + 128],
                            start=(k == 0),
                            stop=(k == 1),
                        )

        def tanh(i):
            th[i] = work.tile([P, 2, P, 4], F32, name="th", bufs=2)
            for gg in range(2):
                nc.scalar.activation(out=th[i][:, gg], in_=y1[i, gg][:].rearrange("p t r -> p r t"), func=ACT.Tanh)

        def mul_g(i):
            hg[i] = work.tile([P, 2, P, 4], BF16, name="hg", bufs=2, align_bytes=64)
            nc.vector.tensor_tensor(
                out=hg[i][:], in0=th[i][:], in1=g_col[:].unsqueeze(2).to_broadcast([P, 2, P, 4]), op=ALU.mult
            )

        def quant_h(i):
            nc.vector.quantize_mx(out=hc[i][:].bitcast(FP8X4), scales=hsc[i][:], in_=hg[i][:].rearrange("p g r t -> p (g r t)"))

        acc = {}

        def mm2(i, h, nh):
            acc[i, h, nh] = psum.tile([P, 512], F32, name="acc", bufs=4)
            cols = slice(512 * nh, 512 * nh + 512)
            for gg in range(2):
                ks = slice(128 * gg, 128 * gg + 128)
                nc.tensor.matmul_mx(
                    out=acc[i, h, nh][:],
                    lhsT=hc[i][:, ks].bitcast(FP8X4),
                    lhsT_scale=hsc[i][:, ks],
                    rhs=whc[h][:, gg, cols].bitcast(FP8X4),
                    rhs_scale=whs[h][:, gg, cols],
                    start=(gg == 0),
                    stop=(gg == 1),
                )

        def flip(i, nh):
            cols = slice(512 * nh, 512 * nh + 512)
            nc.vector.scalar_tensor_tensor(
                out=cs[i // 2][:, i % 2, cols], in0=ms[i // 2][:, i % 2, cols], scalar=0.5, in1=acc[i, 0, nh][:], op0=ALU.subtract, op1=ALU.mult
            )

        def sigm(q, r):
            nc.scalar.activation(out=sg[q][:, r], in_=cs[q][:, r], func=ACT.Sigmoid, scale=2.0)

        dt = {}

        def diff(i, nh):
            cols = slice(512 * nh, 512 * nh + 512)
            nc.vector.tensor_tensor(
                out=dt[i // 2][:, i % 2, cols], in0=acc[i, 1, nh][:], in1=xs[i // 2][:, i % 2, cols], op=ALU.subtract
            )

        def log(q, r):
            nc.scalar.activation(out=sg[q][:, r], in_=sg[q][:, r], func=ACT.Ln, bias=LN_FLOOR)

        def sqr(q, r):
            nc.scalar.activation(out=dt[q][:, r], in_=dt[q][:, r], func=ACT.Square)

        def mini(q, r, c=slice(0, D)):
            nc.vector.scalar_tensor_tensor(out=cs[q][:, r, c], in0=cs[q][:, r, c], scalar=2.0, in1=sg[q][:, r, c], op0=ALU.mult, op1=ALU.min)

        def fin(q, r, c=slice(0, D)):
            nc.vector.scalar_tensor_tensor(out=dt[q][:, r, c], in0=dt[q][:, r, c], scalar=2.0, in1=cs[q][:, r, c], op0=ALU.mult, op1=ALU.subtract)
            rows = slice((2 * q + r.start) * P, (2 * q + r.stop) * P)
            nc.sync.dma_start(out=out[rows, c].rearrange("(r p) d -> p r d", p=P), in_=dt[q][:, r, c])

        def ok(i):
            return 0 <= i < NT

        ALL = slice(0, 2)
        ONE = (slice(0, 1), slice(1, 2))
        tiles_of = [(), (0,), (1,), (2, 3), (4, 5), (6, 7)]
        W = [[(widen, k, p) for p in range(2)] for k in range(8)]
        I = [[(interleave, k, p) for p in range(2)] for k in range(8)]
        PLAN = {'seq': [('i', 0), ('w', 1), ('i', 1), ('w', 2), ('w', 4), ('w', 3), ('i', 2), ('w', 5), ('i', 3), ('i', 5), ('i', 4), ('w', 6), ('w', 7), ('i', 6), ('i', 7)], 'nA': [0, 2, 3, 4, 2, 5, 3, 0], 'nB': [1, 1, 2, 1, 1, 2, 2, 2, 2, 3], 'qA': {7: [2, 3], 5: [1], 3: [0]}, 'qB': {3: [4], 4: [5], 8: [6]}, 'qC': ((), (7,)), 'kT': 5, 'late': 6, 'lag': 2}
        todo = W[0][1:]
        for kind, k in PLAN["seq"]:
            if kind == "w":
                todo += W[k]
            elif kind == "i":
                todo += I[k]
        todo += [(sigm, q, ALL) for q in range(NP)]
        pos = [0]

        def scalar_work(count):
            for f, a, b in todo[pos[0] : pos[0] + count]:
                f(a, b)
            pos[0] += count

        NK = len(pieces)
        LATE = PLAN["late"]
        for k in range(NK + 2):
            if k == 0:
                widen(0, 0)
                spread_s(0)
                spread_s(1)
            scalar_work(PLAN["nA"][k])
            if k < NK:
                mask_m(k)
            if 1 <= k <= NK:
                add_ab(k - 1)
            if k < NK:
                mask_n(k)
            if 1 <= k <= NK:
                mul_s(k - 1)
                for i in tiles_of[k - 1]:
                    turn(i)
            if k < NK:
                prod_a(k)
            if 2 <= k:
                for i in tiles_of[k - 2]:
                    if i < LATE:
                        quant_x(i)
            if k == 3:
                for t in range(4):
                    permute_we(t)
            if k == 4:
                for t in range(4):
                    permute_ws(t)
            for q in PLAN["qA"].get(k, []):
                quant_w(q)
            if k < NK:
                prod_b(k)
            if k == PLAN["kT"]:
                mm1(0)
                tanh(0)
                mm1(1)

        LAG = PLAN["lag"]
        for j in range(NT + LAG):
            if ok(j + 1):
                tanh(j + 1)
            if LATE + j < NT:
                quant_x(LATE + j)
            if ok(j + 2):
                mm1(j + 2)
            if ok(j):
                mul_g(j)
            if ok(j - LAG):
                flip(j - LAG, 0)
            if ok(j):
                quant_h(j)
            if ok(j - LAG):
                flip(j - LAG, 1)
            if ok(j):
                mm2(j, 0, 0)
                mm2(j, 0, 1)
            for q in PLAN["qB"].get(j, []):
                if q in V_WI:
                    interleave(q, 0)
                    interleave(q, 1)
                quant_w(q)
            scalar_work(PLAN["nB"][j])
        scalar_work(len(todo))
        for q in range(NP):
            dt[q] = work.tile([P, 2, D], F32, name="slab", bufs=NP)
        for q in PLAN["qC"][0]:
            quant_w(q)
        for i in range(NT):
            mm2(i, 1, 0)
            diff(i, 0)
        for q in PLAN["qC"][1]:
            quant_w(q)
        for i in range(NT):
            mm2(i, 1, 1)
            diff(i, 1)
        for q in range(NP):
            for r in ONE:
                log(q, r)
                sqr(q, r)
        for q in range(NP):
            mini(q, ONE[0])
            if q:
                fin(q - 1, ONE[1])
            if q < NP - 1:
                mini(q, ONE[1])
                fin(q, ONE[0])
        halves = (slice(0, D // 2), slice(D // 2, D))
        mini(NP - 1, ONE[1], halves[0])
        fin(NP - 1, ONE[0])
        mini(NP - 1, ONE[1], halves[1])
        for c in (halves[0], slice(D // 2, 3 * D // 4), slice(3 * D // 4, D)):
            fin(NP - 1, ONE[1], c)
